import numpy as np
CORES = [97,101,225,229,353,357,481,485]
N = 8
TK = 64
def setup_inputs(rng):
    return {"b": rng.standard_normal((N, 128, TK), dtype=np.float32), "l": (rng.standard_normal((N, 128, N * 128), dtype=np.float32) / 16)}
def setup_inputs_big(rng):
    d = setup_inputs(rng)
    for k in ("b",): d[k] = (d[k].astype(np.float32) * 1048576.0).astype(d[k].dtype)
    return d
def setup_inputs_small(rng):
    d = setup_inputs(rng)
    for k in ("b",): d[k] = (d[k].astype(np.float32) * (1 / 1048576.0)).astype(d[k].dtype)
    return d
def setup_inputs_apart(rng):
    d = setup_inputs(rng)
    f = (10.0 ** rng.permutation(np.linspace(-1.5, 1.5, N))).astype(np.float32).reshape(N, 1, 1)
    for k in ("b",): d[k] = (d[k].astype(np.float32) * f).astype(d[k].dtype)
    return d
def reference(b, l):
    B, L = b.astype(np.float64), l.astype(np.float64)
    y = np.zeros((N, 128, TK))
    for r in range(N):
        acc = B[r].copy()
        for s in range(r):
            acc -= L[r][:, 128 * s:128 * s + 128].T @ y[s]
        y[r] = acc
    return {"y": y.astype(np.float32)}

@@ -1,0 +1,154 @@
+from concourse.bass import DstId, RemoteDMATransfer
+from concourse.mybir import AluOpType
+
+N, W, TS = 8, 64, 128
+
+SCRATCH = {"Y": ("sbuf", [128, N * W], "float32")}
+for _r in range(1, N):
+    SCRATCH["R%d" % _r] = ("sbuf", [128, W + TS * _r], "float32")
+    SCRATCH["acc%d" % _r] = ("psum", [128, 512], "float32")
+
+MSGS = [
+    (0, "Y", 0, 64, [1, 3, 2, 7, 6]),
+    (1, "R1", 0, 192, [0, 3, 2]),
+    (2, "R2", 0, 320, [3, 1]),
+    (3, "R3", 0, 448, [1]),
+    (4, "R4", 0, 576, [5, 7, 6]),
+    (5, "R5", 0, 704, [7, 6]),
+    (6, "R6", 0, 832, [7]),
+    (0, "Y", 64, 128, [7, 6]),
+    (1, "Y", 128, 192, [7, 6]),
+    (1, "Y", 192, 256, [7, 6]),
+    (2, "Y", 0, 192, [5, 4]),
+    (3, "Y", 192, 256, [5, 4]),
+]
+
+ORDER = {
+    0: [(1, 0)],
+    1: [(1, 0), (2, 0), (2, 1), (3, 0), (3, 1), (3, 2)],
+    2: [(2, 0), (1, 0), (2, 1)],
+    3: [(3, 0), (2, 0), (1, 0), (2, 1), (3, 1), (3, 2)],
+    4: [(4, 0), (4, 1), (4, 2), (4, 3)],
+    5: [(4, 0), (4, 1), (4, 2), (5, 0), (5, 1), (5, 2), (4, 3), (5, 3), (5, 4)],
+    6: [(6, 0), (6, 1), (4, 0), (4, 1), (5, 0), (5, 1), (4, 2), (5, 2), (6, 2),
+        (4, 3), (5, 3), (6, 3), (5, 4), (6, 4), (6, 5)],
+    7: [(7, 0), (6, 0), (7, 1), (6, 1), (4, 0), (4, 1), (5, 0), (5, 1), (4, 2), (5, 2), (6, 2), (7, 2),
+        (4, 3), (5, 3), (6, 3), (5, 4), (6, 4), (7, 3), (6, 5), (7, 4), (7, 5), (7, 6)],
+}
+
+SEMAPHORES = (["ld", "st", "sent"] + ["m%d" % k for k in range(len(MSGS))]
+              + ["p%d" % r for r in range(1, N)] + ["v%d" % r for r in range(1, N)])
+
+
+def _items(buf, lo, hi):
+    if buf == "Y":
+        return ["y%d" % s for s in range(lo // W, hi // W)]
+    return [buf]
+
+
+def _ones(mask):
+    return bin(mask).count("1")
+
+
+def _groups(topo, cores, src, dests):
+    c = cores[src]
+    on = [d for d in dests if (topo.host(cores[d]), topo.chip(cores[d])) == (topo.host(c), topo.chip(c))]
+    off = [d for d in dests if d not in on]
+    m_off = 0
+    if off:
+        m_off = topo.mask(c, cores[off[0]])
+        for d in off:
+            m_off &= topo.mask(c, cores[d])
+    out = []
+    if on:
+        m_on = topo.mask(c, cores[on[0]]) & ~m_off
+        out.append((m_on, on))
+    if off:
+        out.append((m_off, off))
+    return out
+
+
+def rank_program(g, core, T, topo):
+    rank = T.rank_of(core)
+    if rank is None:
+        return
+    cores = T.cores
+    sem = T.sem
+    have = {}
+
+    if rank == 0:
+        g.sync.dma_start(T.Y[:, 0:W], T.b[:, :]).then_inc(sem.ld, 16)
+        have["y0"] = (sem.ld, 16)
+        g.scalar.dma_start(T.y[:, :], T.b[:, :]).then_inc(sem.st, 16)
+        g.scalar.wait_ge(sem.st, 16)
+    else:
+        own = T["R%d" % rank]
+        g.sync.dma_start(own[:, 0:W], T.b[:, :]).then_inc(sem.ld, 16)
+        g.scalar.dma_start(own[:, W:W + TS * rank], T.l[:, 0:TS * rank]).then_inc(sem.ld, 16)
+        have["R%d" % rank] = (sem.ld, 32)
+
+    for k, (src, buf, lo, hi, dests) in enumerate(MSGS):
+        if rank in dests:
+            for mask, ranks in _groups(topo, cores, src, dests):
+                if rank in ranks:
+                    for it in _items(buf, lo, hi):
+                        have[it] = (sem["m%d" % k], _ones(mask))
+    order = ORDER[rank]
+    rows = sorted(set(r for r, _ in order))
+    for r in rows:
+        have["y%d" % r] = (sem["v%d" % r], 1)
+
+    def waiter(queue):
+        seen = set()
+
+        def wait(item):
+            if item not in seen:
+                seen.add(item)
+                s, n = have[item]
+                queue.wait_ge(s, n)
+        return wait
+
+    wt = waiter(g.tensor)
+    done = dict((r, 0) for r in rows)
+    for r, s in order:
+        wt("R%d" % r)
+        wt("y%d" % s)
+        done[r] += 1
+        mm = g.tensor.matmul(T["acc%d" % r][:, 0:W], T["R%d" % r][:, W + TS * s:W + TS * (s + 1)],
+                             T.Y[:, W * s:W * (s + 1)], done[r] == 1, done[r] == r)
+        if done[r] == r:
+            mm.then_inc(sem["p%d" % r], 1)
+
+    wv = waiter(g.vector)
+    for r in rows:
+        wv("R%d" % r)
+        g.vector.wait_ge(sem["p%d" % r], 1)
+        g.vector.tensor_tensor(T.Y[:, W * r:W * (r + 1)], T["R%d" % r][:, 0:W], T["acc%d" % r][:, 0:W],
+                               AluOpType.subtract).then_inc(sem["v%d" % r], 1)
+
+    if rank > 0:
+        s, n = have["y%d" % rank]
+        g.sync.wait_ge(s, n)
+        g.sync.dma_start(T.y[:, :], T.Y[:, W * rank:W * (rank + 1)]).then_inc(sem.st, 16)
+        g.sync.wait_ge(sem.st, 16)
+
+    wg = waiter(g)
+    sent = 0
+    for k, (src, buf, lo, hi, dests) in enumerate(MSGS):
+        if src != rank:
+            continue
+        for it in _items(buf, lo, hi):
+            wg(it)
+        ap = T[buf][:, lo:hi]
+        transfers = []
+        for mask, ranks in _groups(topo, cores, src, dests):
+            ids = []
+            for d in ranks:
+                rid, pid = topo.addr(cores[d], core)
+                ids.append(DstId(rid=rid, pnc=pid))
+            transfers.append(RemoteDMATransfer(dst_ids=ids, dma_engine_mask=mask, remote_sem=sem["m%d" % k],
+                                               srcs=[ap], dsts=[ap for _ in ranks], alu_op=0))
+            sent += _ones(mask)
+        g.remote_dma_fused(transfers, local_sem=sem.sent)
+    if sent:
+        g.wait_ge(sem.sent, sent)

@@ -9,18 +9,24 @@ for _r in range(1, N):
     SCRATCH["acc%d" % _r] = ("psum", [128, 512], "float32")
 
 MSGS = [
-    (0, "Y", 0, 64, [1, 3, 2, 7, 6]),
-    (1, "R1", 0, 192, [0, 3, 2]),
-    (2, "R2", 0, 320, [3, 1]),
-    (3, "R3", 0, 448, [1]),
-    (4, "R4", 0, 576, [5, 7, 6]),
-    (5, "R5", 0, 704, [7, 6]),
-    (6, "R6", 0, 832, [7]),
-    (0, "Y", 64, 128, [7, 6]),
-    (1, "Y", 128, 192, [7, 6]),
-    (1, "Y", 192, 256, [7, 6]),
-    (2, "Y", 0, 192, [5, 4]),
-    (3, "Y", 192, 256, [5, 4]),
+    (0, "Y", [(0, 64, [1, 2, 3, 7, 6])]),
+    (1, "R1", [(0, 192, [0, 2, 3])]),
+    (2, "R2", [(0, 320, [3, 1])]),
+    (3, "R3", [(0, 448, [1])]),
+    (4, "R4", [(0, 288, [6]), (288, 576, [7])]),
+    (4, "R4", [(0, 576, [5])]),
+    (5, "R5", [(0, 352, [6]), (352, 704, [7])]),
+    (6, "R6", [(0, 832, [7])]),
+    (6, "R4", [(0, 288, [7])]),
+    (7, "R4", [(288, 576, [6])]),
+    (6, "R5", [(0, 352, [7])]),
+    (7, "R5", [(352, 704, [6])]),
+    (0, "Y", [(64, 128, [7, 6])]),
+    (1, "Y", [(128, 192, [7, 6])]),
+    (1, "Y", [(192, 256, [7, 6])]),
+    (3, "Y", [(0, 64, [5, 4])]),
+    (2, "Y", [(64, 192, [5, 4])]),
+    (3, "Y", [(192, 256, [5, 4])]),
 ]
 
 ORDER = {
@@ -29,10 +35,10 @@ ORDER = {
     2: [(2, 0), (1, 0), (2, 1)],
     3: [(3, 0), (2, 0), (1, 0), (2, 1), (3, 1), (3, 2)],
     4: [(4, 0), (4, 1), (4, 2), (4, 3)],
-    5: [(4, 0), (4, 1), (4, 2), (5, 0), (5, 1), (5, 2), (4, 3), (5, 3), (5, 4)],
-    6: [(6, 0), (6, 1), (4, 0), (4, 1), (5, 0), (5, 1), (4, 2), (5, 2), (6, 2),
+    5: [(4, 0), (5, 0), (4, 1), (4, 2), (5, 1), (5, 2), (4, 3), (5, 3), (5, 4)],
+    6: [(6, 0), (4, 0), (6, 1), (4, 1), (5, 0), (5, 1), (4, 2), (5, 2), (6, 2),
         (4, 3), (5, 3), (6, 3), (5, 4), (6, 4), (6, 5)],
-    7: [(7, 0), (6, 0), (7, 1), (6, 1), (4, 0), (4, 1), (5, 0), (5, 1), (4, 2), (5, 2), (6, 2), (7, 2),
+    7: [(7, 0), (6, 0), (4, 0), (7, 1), (6, 1), (4, 1), (5, 0), (5, 1), (4, 2), (5, 2), (6, 2), (7, 2),
         (4, 3), (5, 3), (6, 3), (5, 4), (6, 4), (7, 3), (6, 5), (7, 4), (7, 5), (7, 6)],
 }
 
@@ -50,21 +56,28 @@ def _ones(mask):
     return bin(mask).count("1")
 
 
-def _groups(topo, cores, src, dests):
+def _transfers(topo, cores, src, parts):
     c = cores[src]
-    on = [d for d in dests if (topo.host(cores[d]), topo.chip(cores[d])) == (topo.host(c), topo.chip(c))]
-    off = [d for d in dests if d not in on]
+
+    def near(d):
+        return (topo.host(cores[d]), topo.chip(cores[d])) == (topo.host(c), topo.chip(c))
+
     m_off = 0
-    if off:
-        m_off = topo.mask(c, cores[off[0]])
-        for d in off:
+    far = [d for _, _, dests in parts for d in dests if not near(d)]
+    if far:
+        m_off = topo.mask(c, cores[far[0]])
+        for d in far:
             m_off &= topo.mask(c, cores[d])
+    bits = [1 << i for i in range(m_off.bit_length()) if (m_off >> i) & 1]
+    share = len(bits) // len(parts)
     out = []
-    if on:
-        m_on = topo.mask(c, cores[on[0]]) & ~m_off
-        out.append((m_on, on))
-    if off:
-        out.append((m_off, off))
+    for j, (lo, hi, dests) in enumerate(parts):
+        on = [d for d in dests if near(d)]
+        off = [d for d in dests if not near(d)]
+        if on:
+            out.append((topo.mask(c, cores[on[0]]) & ~m_off, lo, hi, on))
+        if off:
+            out.append((sum(bits[j * share:(j + 1) * share]), lo, hi, off))
     return out
 
 
@@ -75,28 +88,29 @@ def rank_program(g, core, T, topo):
     cores = T.cores
     sem = T.sem
     have = {}
+    piece = {}
 
     if rank == 0:
         g.sync.dma_start(T.Y[:, 0:W], T.b[:, :]).then_inc(sem.ld, 16)
-        have["y0"] = (sem.ld, 16)
+        have["y0"] = [(sem.ld, 16)]
         g.scalar.dma_start(T.y[:, :], T.b[:, :]).then_inc(sem.st, 16)
         g.scalar.wait_ge(sem.st, 16)
     else:
         own = T["R%d" % rank]
         g.sync.dma_start(own[:, 0:W], T.b[:, :]).then_inc(sem.ld, 16)
         g.scalar.dma_start(own[:, W:W + TS * rank], T.l[:, 0:TS * rank]).then_inc(sem.ld, 16)
-        have["R%d" % rank] = (sem.ld, 32)
+        have["R%d" % rank] = [(sem.ld, 32)]
 
-    for k, (src, buf, lo, hi, dests) in enumerate(MSGS):
-        if rank in dests:
-            for mask, ranks in _groups(topo, cores, src, dests):
-                if rank in ranks:
-                    for it in _items(buf, lo, hi):
-                        have[it] = (sem["m%d" % k], _ones(mask))
+    for k, (src, buf, parts) in enumerate(MSGS):
+        for mask, lo, hi, ranks in _transfers(topo, cores, src, parts):
+            if rank in ranks:
+                piece[(buf, lo, hi)] = (sem["m%d" % k], _ones(mask))
+                for it in _items(buf, lo, hi):
+                    have.setdefault(it, []).append((sem["m%d" % k], _ones(mask)))
     order = ORDER[rank]
     rows = sorted(set(r for r, _ in order))
     for r in rows:
-        have["y%d" % r] = (sem["v%d" % r], 1)
+        have["y%d" % r] = [(sem["v%d" % r], 1)]
 
     def waiter(queue):
         seen = set()
@@ -104,8 +118,8 @@ def rank_program(g, core, T, topo):
         def wait(item):
             if item not in seen:
                 seen.add(item)
-                s, n = have[item]
-                queue.wait_ge(s, n)
+                for s, n in have[item]:
+                    queue.wait_ge(s, n)
         return wait
 
     wt = waiter(g.tensor)
@@ -127,21 +141,25 @@ def rank_program(g, core, T, topo):
                                AluOpType.subtract).then_inc(sem["v%d" % r], 1)
 
     if rank > 0:
-        s, n = have["y%d" % rank]
-        g.sync.wait_ge(s, n)
+        g.sync.wait_ge(sem["v%d" % rank], 1)
         g.sync.dma_start(T.y[:, :], T.Y[:, W * rank:W * (rank + 1)]).then_inc(sem.st, 16)
         g.sync.wait_ge(sem.st, 16)
 
     wg = waiter(g)
     sent = 0
-    for k, (src, buf, lo, hi, dests) in enumerate(MSGS):
+    for k, (src, buf, parts) in enumerate(MSGS):
         if src != rank:
             continue
-        for it in _items(buf, lo, hi):
-            wg(it)
-        ap = T[buf][:, lo:hi]
+        for lo, hi, _ in parts:
+            if (buf, lo, hi) in piece:
+                s, n = piece[(buf, lo, hi)]
+                g.wait_ge(s, n)
+            else:
+                for it in _items(buf, lo, hi):
+                    wg(it)
         transfers = []
-        for mask, ranks in _groups(topo, cores, src, dests):
+        for mask, lo, hi, ranks in _transfers(topo, cores, src, parts):
+            ap = T[buf][:, lo:hi]
             ids = []
             for d in ranks:
                 rid, pid = topo.addr(cores[d], core)

@@ -7,6 +7,9 @@ SCRATCH = {"Y": ("sbuf", [128, N * W], "float32")}
 for _r in range(1, N):
     SCRATCH["R%d" % _r] = ("sbuf", [128, W + TS * _r], "float32")
     SCRATCH["acc%d" % _r] = ("psum", [128, 512], "float32")
+SCRATCH["ident"] = ("sbuf", [128, TS], "float32")
+SCRATCH["L6T"] = ("sbuf", [128, 3 * TS], "float32")
+SCRATCH["M7"] = ("sbuf", [128, 3 * TS], "float32")
 
 MSGS = [
     (0, "Y", [(0, 64, [1, 2, 3, 7, 6])]),
@@ -22,7 +25,8 @@ MSGS = [
     (6, "R5", [(0, 352, [7])]),
     (7, "R5", [(352, 704, [6])]),
     (0, "Y", [(64, 128, [7, 6])]),
-    (1, "Y", [(128, 192, [7, 6])]),
+    (1, "Y", [(128, 192, [7])]),
+    (7, "Y", [(128, 192, [6])]),
     (1, "Y", [(192, 256, [7, 6])]),
     (3, "Y", [(0, 64, [5, 4])]),
     (2, "Y", [(64, 192, [5, 4])]),
@@ -38,11 +42,12 @@ ORDER = {
     5: [(4, 0), (5, 0), (4, 1), (4, 2), (5, 1), (5, 2), (4, 3), (5, 3), (5, 4)],
     6: [(6, 0), (4, 0), (6, 1), (4, 1), (5, 0), (5, 1), (4, 2), (5, 2), (6, 2),
         (4, 3), (5, 3), (6, 3), (5, 4), (6, 4), (6, 5)],
-    7: [(7, 0), (6, 0), (4, 0), (7, 1), (6, 1), (4, 1), (5, 0), (5, 1), (4, 2), (5, 2), (6, 2), (7, 2),
-        (4, 3), (5, 3), (6, 3), (5, 4), (6, 4), (7, 3), (6, 5), (7, 4), (7, 5), (7, 6)],
+    7: [("T", 3), ("T", 4), ("T", 5), (7, 0), (6, 0), ("P", 3), ("P", 4), ("P", 5), (7, 1), (6, 1),
+        (4, 0), (4, 1), (5, 0), (5, 1), (6, 2), (7, 2), (4, 2), (5, 2), (7, 6),
+        (4, 3), (5, 3), ("F", 3), (5, 4), ("F", 4), ("F", 5)],
 }
 
-SEMAPHORES = (["ld", "st", "sent"] + ["m%d" % k for k in range(len(MSGS))]
+SEMAPHORES = (["ld", "st", "sent", "id0", "id1", "tp", "lt", "pp", "mf"] + ["m%d" % k for k in range(len(MSGS))]
               + ["p%d" % r for r in range(1, N)] + ["v%d" % r for r in range(1, N)])
 
 
@@ -108,9 +113,21 @@ def rank_program(g, core, T, topo):
                 for it in _items(buf, lo, hi):
                     have.setdefault(it, []).append((sem["m%d" % k], _ones(mask)))
     order = ORDER[rank]
-    rows = sorted(set(r for r, _ in order))
+    sums = [(7, op[1]) if op[0] == "F" else op for op in order if op[0] not in ("T", "P")]
+    size = {}
+    for r, _ in sums:
+        size[r] = size.get(r, 0) + 1
+    rows, cnt = [], {}
+    for r, _ in sums:
+        cnt[r] = cnt.get(r, 0) + 1
+        if cnt[r] == size[r]:
+            rows.append(r)
     for r in rows:
         have["y%d" % r] = [(sem["v%d" % r], 1)]
+    have["ident"] = [(sem.id1, 1)]
+    have["L6T"] = [(sem.lt, 1)]
+    have["M7"] = [(sem.mf, 1)]
+    fold = any(op[0] == "F" for op in order)
 
     def waiter(queue):
         seen = set()
@@ -122,18 +139,47 @@ def rank_program(g, core, T, topo):
                     queue.wait_ge(s, n)
         return wait
 
+    def tile(r, s):
+        return T["R%d" % r][:, W + TS * s:W + TS * (s + 1)]
+
     wt = waiter(g.tensor)
     done = dict((r, 0) for r in rows)
-    for r, s in order:
-        wt("R%d" % r)
+    for op in order:
+        if op[0] == "T":
+            blk = slice(TS * (op[1] - 3), TS * (op[1] - 2))
+            wt("R6")
+            wt("ident")
+            g.tensor.matmul(T.acc1[:, blk], tile(6, op[1]), T.ident[:, :], True, True).then_inc(sem.tp, 1)
+            continue
+        if op[0] == "P":
+            blk = slice(TS * (op[1] - 3), TS * (op[1] - 2))
+            wt("L6T")
+            wt("R7")
+            g.tensor.matmul(T.acc2[:, blk], T.L6T[:, blk], tile(7, 6), True, True).then_inc(sem.pp, 1)
+            continue
+        if op[0] == "F":
+            r, s = 7, op[1]
+            wt("M7")
+            lhs = T.M7[:, TS * (s - 3):TS * (s - 2)]
+        else:
+            r, s = op
+            wt("R%d" % r)
+            lhs = tile(r, s)
         wt("y%d" % s)
         done[r] += 1
-        mm = g.tensor.matmul(T["acc%d" % r][:, 0:W], T["R%d" % r][:, W + TS * s:W + TS * (s + 1)],
-                             T.Y[:, W * s:W * (s + 1)], done[r] == 1, done[r] == r)
-        if done[r] == r:
+        mm = g.tensor.matmul(T["acc%d" % r][:, 0:W], lhs, T.Y[:, W * s:W * (s + 1)], done[r] == 1, done[r] == size[r])
+        if done[r] == size[r]:
             mm.then_inc(sem["p%d" % r], 1)
 
     wv = waiter(g.vector)
+    if fold:
+        g.vector.memset(T.ident[:, :], 1.0).then_inc(sem.id0, 1)
+        g.vector.wait_ge(sem.tp, 3)
+        g.vector.tensor_copy(T.L6T[:, :], T.acc1[:, 0:3 * TS]).then_inc(sem.lt, 1)
+        wv("R7")
+        g.vector.wait_ge(sem.pp, 3)
+        g.vector.tensor_tensor(T.M7[:, :], T.R7[:, W + 3 * TS:W + 6 * TS], T.acc2[:, 0:3 * TS],
+                               AluOpType.subtract).then_inc(sem.mf, 1)
     for r in rows:
         wv("R%d" % r)
         g.vector.wait_ge(sem["p%d" % r], 1)
@@ -145,6 +191,9 @@ def rank_program(g, core, T, topo):
         g.sync.dma_start(T.y[:, :], T.Y[:, W * rank:W * (rank + 1)]).then_inc(sem.st, 16)
         g.sync.wait_ge(sem.st, 16)
 
+    if fold:
+        g.wait_ge(sem.id0, 1)
+        g.affine_select(T.ident[:, :], T.ident[:, :], [[-1, TS]], AluOpType.is_equal, 0.0, 0, 1).then_inc(sem.id1, 1)
     wg = waiter(g)
     sent = 0
     for k, (src, buf, parts) in enumerate(MSGS):

@@ -3,11 +3,12 @@ from concourse.mybir import AluOpType
 
 N, W, TS = 8, 64, 128
 
-SCRATCH = {"Y": ("sbuf", [128, N * W], "float32")}
+SCRATCH = {"Y": ("sbuf", [128, N * W], "float32"), "acc0": ("psum", [128, 512], "float32")}
 for _r in range(1, N):
     SCRATCH["R%d" % _r] = ("sbuf", [128, W + TS * _r], "float32")
     SCRATCH["acc%d" % _r] = ("psum", [128, 512], "float32")
 SCRATCH["ident"] = ("sbuf", [128, TS], "float32")
+SCRATCH["L5T"] = ("sbuf", [128, 3 * TS], "float32")
 SCRATCH["L6T"] = ("sbuf", [128, 3 * TS], "float32")
 SCRATCH["M7"] = ("sbuf", [128, 3 * TS], "float32")
 
@@ -16,38 +17,41 @@ MSGS = [
     (1, "R1", [(0, 192, [0, 2, 3])]),
     (2, "R2", [(0, 320, [3, 1])]),
     (3, "R3", [(0, 448, [1])]),
-    (4, "R4", [(0, 288, [6]), (288, 576, [7])]),
+    (3, "R3", [(0, 448, [2])]),
+    (4, "R4", [(0, 288, [7]), (288, 576, [6])]),
     (4, "R4", [(0, 576, [5])]),
-    (5, "R5", [(0, 352, [6]), (352, 704, [7])]),
-    (6, "R6", [(0, 832, [7])]),
-    (6, "R4", [(0, 288, [7])]),
-    (7, "R4", [(288, 576, [6])]),
-    (6, "R5", [(0, 352, [7])]),
-    (7, "R5", [(352, 704, [6])]),
+    (5, "R5", [(0, 352, [7]), (352, 704, [6])]),
+    (6, "R6", [(0, 448, [7])]),
+    (6, "L6T", [(0, 384, [7])]),
+    (6, "R4", [(288, 576, [7])]),
+    (7, "R4", [(0, 288, [6])]),
+    (6, "R5", [(352, 704, [7])]),
+    (7, "R5", [(0, 352, [6])]),
     (0, "Y", [(64, 128, [7, 6])]),
     (1, "Y", [(128, 192, [7])]),
     (7, "Y", [(128, 192, [6])]),
     (1, "Y", [(192, 256, [7, 6])]),
     (3, "Y", [(0, 64, [5, 4])]),
-    (2, "Y", [(64, 192, [5, 4])]),
-    (3, "Y", [(192, 256, [5, 4])]),
+    (2, "Y", [(64, 192, [5])]),
+    (5, "Y", [(64, 192, [4])]),
+    (2, "Y", [(192, 256, [5])]),
+    (3, "Y", [(192, 256, [4])]),
 ]
+SPARE = (4,)
 
 ORDER = {
     0: [(1, 0)],
     1: [(1, 0), (2, 0), (2, 1), (3, 0), (3, 1), (3, 2)],
-    2: [(2, 0), (1, 0), (2, 1)],
+    2: [(2, 0), (1, 0), (2, 1), (3, 0), (3, 1), (3, 2)],
     3: [(3, 0), (2, 0), (1, 0), (2, 1), (3, 1), (3, 2)],
     4: [(4, 0), (4, 1), (4, 2), (4, 3)],
     5: [(4, 0), (5, 0), (4, 1), (4, 2), (5, 1), (5, 2), (4, 3), (5, 3), (5, 4)],
-    6: [(6, 0), (4, 0), (6, 1), (4, 1), (5, 0), (5, 1), (4, 2), (5, 2), (6, 2),
-        (4, 3), (5, 3), (6, 3), (5, 4), (6, 4), (6, 5)],
-    7: [("T", 3), ("T", 4), ("T", 5), (7, 0), (6, 0), ("P", 3), ("P", 4), ("P", 5), (7, 1), (6, 1),
-        (4, 0), (4, 1), (5, 0), (5, 1), (6, 2), (7, 2), (4, 2), (5, 2), (7, 6),
-        (4, 3), (5, 3), ("F", 3), (5, 4), ("F", 4), ("F", 5)],
+    6: [],
+    7: [],
 }
 
-SEMAPHORES = (["ld", "st", "sent", "id0", "id1", "tp", "lt", "pp", "mf"] + ["m%d" % k for k in range(len(MSGS))]
+SEMAPHORES = (["ld", "st", "sent", "id0", "id1", "tp", "tq", "tr", "lt", "lu", "lv", "pp", "qq", "qr", "hf", "mf", "mg"]
+              + ["m%d" % k for k in range(len(MSGS))]
               + ["p%d" % r for r in range(1, N)] + ["v%d" % r for r in range(1, N)])
 
 
@@ -61,7 +65,7 @@ def _ones(mask):
     return bin(mask).count("1")
 
 
-def _transfers(topo, cores, src, parts):
+def _transfers(topo, cores, src, parts, spare):
     c = cores[src]
 
     def near(d):
@@ -69,6 +73,8 @@ def _transfers(topo, cores, src, parts):
 
     m_off = 0
     far = [d for _, _, dests in parts for d in dests if not near(d)]
+    if spare:
+        far = [d for d in range(len(cores)) if not near(d) and topo.may_write(c, cores[d])]
     if far:
         m_off = topo.mask(c, cores[far[0]])
         for d in far:
@@ -107,27 +113,26 @@ def rank_program(g, core, T, topo):
         have["R%d" % rank] = [(sem.ld, 32)]
 
     for k, (src, buf, parts) in enumerate(MSGS):
-        for mask, lo, hi, ranks in _transfers(topo, cores, src, parts):
+        for mask, lo, hi, ranks in _transfers(topo, cores, src, parts, k in SPARE):
             if rank in ranks:
                 piece[(buf, lo, hi)] = (sem["m%d" % k], _ones(mask))
                 for it in _items(buf, lo, hi):
                     have.setdefault(it, []).append((sem["m%d" % k], _ones(mask)))
     order = ORDER[rank]
-    sums = [(7, op[1]) if op[0] == "F" else op for op in order if op[0] not in ("T", "P")]
     size = {}
-    for r, _ in sums:
+    for r, _ in order:
         size[r] = size.get(r, 0) + 1
     rows, cnt = [], {}
-    for r, _ in sums:
+    for r, _ in order:
         cnt[r] = cnt.get(r, 0) + 1
         if cnt[r] == size[r]:
             rows.append(r)
     for r in rows:
         have["y%d" % r] = [(sem["v%d" % r], 1)]
     have["ident"] = [(sem.id1, 1)]
-    have["L6T"] = [(sem.lt, 1)]
-    have["M7"] = [(sem.mf, 1)]
-    fold = any(op[0] == "F" for op in order)
+    if rank == 6:
+        have["L6T"] = [(sem.lt, 1)]
+    fold = rank >= 6
 
     def waiter(queue):
         seen = set()
@@ -142,49 +147,127 @@ def rank_program(g, core, T, topo):
     def tile(r, s):
         return T["R%d" % r][:, W + TS * s:W + TS * (s + 1)]
 
+    def ycol(s):
+        return T.Y[:, W * s:W * (s + 1)]
+
+    def acc(r):
+        return T["acc%d" % r][:, 0:W]
+
     wt = waiter(g.tensor)
     done = dict((r, 0) for r in rows)
-    for op in order:
-        if op[0] == "T":
-            blk = slice(TS * (op[1] - 3), TS * (op[1] - 2))
-            wt("R6")
-            wt("ident")
-            g.tensor.matmul(T.acc1[:, blk], tile(6, op[1]), T.ident[:, :], True, True).then_inc(sem.tp, 1)
-            continue
-        if op[0] == "P":
-            blk = slice(TS * (op[1] - 3), TS * (op[1] - 2))
-            wt("L6T")
-            wt("R7")
-            g.tensor.matmul(T.acc2[:, blk], T.L6T[:, blk], tile(7, 6), True, True).then_inc(sem.pp, 1)
-            continue
-        if op[0] == "F":
-            r, s = 7, op[1]
-            wt("M7")
-            lhs = T.M7[:, TS * (s - 3):TS * (s - 2)]
-        else:
-            r, s = op
-            wt("R%d" % r)
-            lhs = tile(r, s)
+    for r, s in order:
+        wt("R%d" % r)
         wt("y%d" % s)
         done[r] += 1
-        mm = g.tensor.matmul(T["acc%d" % r][:, 0:W], lhs, T.Y[:, W * s:W * (s + 1)], done[r] == 1, done[r] == size[r])
+        mm = g.tensor.matmul(acc(r), tile(r, s), ycol(s), done[r] == 1, done[r] == size[r])
         if done[r] == size[r]:
             mm.then_inc(sem["p%d" % r], 1)
 
     wv = waiter(g.vector)
-    if fold:
-        g.vector.memset(T.ident[:, :], 1.0).then_inc(sem.id0, 1)
-        g.vector.wait_ge(sem.tp, 3)
-        g.vector.tensor_copy(T.L6T[:, :], T.acc1[:, 0:3 * TS]).then_inc(sem.lt, 1)
-        wv("R7")
-        g.vector.wait_ge(sem.pp, 3)
-        g.vector.tensor_tensor(T.M7[:, :], T.R7[:, W + 3 * TS:W + 6 * TS], T.acc2[:, 0:3 * TS],
-                               AluOpType.subtract).then_inc(sem.mf, 1)
-    for r in rows:
+
+    def finish(r):
         wv("R%d" % r)
         g.vector.wait_ge(sem["p%d" % r], 1)
-        g.vector.tensor_tensor(T.Y[:, W * r:W * (r + 1)], T["R%d" % r][:, 0:W], T["acc%d" % r][:, 0:W],
-                               AluOpType.subtract).then_inc(sem["v%d" % r], 1)
+        g.vector.tensor_tensor(ycol(r), T["R%d" % r][:, 0:W], acc(r), AluOpType.subtract).then_inc(sem["v%d" % r], 1)
+
+    for r in rows:
+        finish(r)
+
+    if fold:
+        te, ve, sub = g.tensor, g.vector, AluOpType.subtract
+        eye = T.ident[:, :]
+        t54T, t43T, t53T = T.L5T[:, 0:TS], T.L5T[:, TS:2 * TS], T.L5T[:, 2 * TS:3 * TS]
+        left4 = [key for key in piece if key[0] == "R4" and key[1] == 0][0]
+        left5 = [key for key in piece if key[0] == "R5" and key[1] == 0][0]
+        right4 = [key for key in piece if key[0] == "R4" and key[2] == W + 4 * TS][0]
+        right5 = [key for key in piece if key[0] == "R5" and key[2] == W + 5 * TS][0]
+        mine = list(range(4, rank + 1))
+        ve.memset(eye, 1.0).then_inc(sem.id0, 1)
+
+        def transposes():
+            wt("ident")
+            te.wait_ge(*piece[right4])
+            te.matmul(T.acc3[:, 0:TS], tile(4, 3), eye, True, True).then_inc(sem.tq, 1)
+            te.wait_ge(*piece[right5])
+            te.matmul(T.acc0[:, 0:TS], tile(5, 4), eye, True, True).then_inc(sem.tr, 1)
+            te.matmul(T.acc3[:, TS:2 * TS], tile(5, 3), eye, True, True).then_inc(sem.tq, 1)
+            ve.wait_ge(sem.tr, 1)
+            ve.tensor_copy(t54T, T.acc0[:, 0:TS]).then_inc(sem.lu, 1)
+            ve.wait_ge(sem.tq, 2)
+            ve.tensor_copy(T.L5T[:, TS:3 * TS], T.acc3[:, 0:2 * TS]).then_inc(sem.lv, 1)
+
+        def fold_tiles(h5, h4, h4_in, m3, m3_in):
+            te.wait_ge(sem.lu, 1)
+            te.matmul(T.acc1[:, 0:TS], t54T, h5, True, True).then_inc(sem.qq, 1)
+            te.wait_ge(sem.lv, 1)
+            te.matmul(T.acc2[:, 0:TS], t53T, h5, True, False)
+            te.wait_ge(sem.hf, 1)
+            te.matmul(T.acc2[:, 0:TS], t43T, h4, False, True).then_inc(sem.qr, 1)
+            ve.wait_ge(sem.qq, 1)
+            ve.tensor_tensor(h4, h4_in, T.acc1[:, 0:TS], sub).then_inc(sem.hf, 1)
+            ve.wait_ge(sem.qr, 1)
+            ve.tensor_tensor(m3, m3_in, T.acc2[:, 0:TS], sub).then_inc(sem.mg, 1)
+
+        wt("R%d" % rank)
+        wv("R%d" % rank)
+        if rank == 6:
+            wt("ident")
+            for s in (3, 4, 5):
+                blk = slice(TS * (s - 3), TS * (s - 2))
+                te.matmul(T.acc1[:, blk], tile(6, s), eye, True, True).then_inc(sem.tp, 1)
+            ve.wait_ge(sem.tp, 3)
+            ve.tensor_copy(T.L6T[:, :], T.acc1[:, 0:3 * TS]).then_inc(sem.lt, 1)
+            wt("y0")
+            te.matmul(acc(6), tile(6, 0), ycol(0), True, False)
+            transposes()
+            wt("L6T")
+            h5, h4, m3 = tile(6, 5), T.M7[:, TS:2 * TS], T.M7[:, 0:TS]
+            fold_tiles(h5, h4, tile(6, 4), m3, tile(6, 3))
+            weights = {4: h4, 5: h5}
+            wt("R4")
+            te.matmul(acc(4), tile(4, 0), ycol(0), True, False)
+            wt("R5")
+            te.matmul(acc(5), tile(5, 0), ycol(0), True, False)
+            wt("y1")
+            for r in mine:
+                te.matmul(acc(r), tile(r, 1), ycol(1), False, False)
+        else:
+            wt("L6T")
+            for s in (3, 4, 5):
+                blk = slice(TS * (s - 3), TS * (s - 2))
+                te.matmul(T.acc2[:, blk], T.L6T[:, blk], tile(7, 6), True, True).then_inc(sem.pp, 1)
+            ve.wait_ge(sem.pp, 3)
+            ve.tensor_tensor(T.M7[:, :], T.R7[:, W + 3 * TS:W + 6 * TS], T.acc2[:, 0:3 * TS], sub).then_inc(sem.mf, 1)
+            wt("y0")
+            te.matmul(acc(7), tile(7, 0), ycol(0), True, False)
+            wt("R6")
+            te.matmul(acc(6), tile(6, 0), ycol(0), True, False)
+            te.wait_ge(*piece[left4])
+            te.matmul(acc(4), tile(4, 0), ycol(0), True, False)
+            te.wait_ge(*piece[left5])
+            te.matmul(acc(5), tile(5, 0), ycol(0), True, False)
+            wt("y1")
+            for r in (5, 6, 7):
+                te.matmul(acc(r), tile(r, 1), ycol(1), False, False)
+            transposes()
+            te.matmul(acc(4), tile(4, 1), ycol(1), False, False)
+            te.wait_ge(sem.mf, 1)
+            m3, h4, h5 = T.M7[:, 0:TS], T.M7[:, TS:2 * TS], T.M7[:, 2 * TS:3 * TS]
+            fold_tiles(h5, h4, h4, m3, m3)
+            weights = {4: h4, 5: h5, 6: tile(7, 6)}
+        wt("y2")
+        for r in mine:
+            mm = te.matmul(acc(r), tile(r, 2), ycol(2), False, r < rank)
+            if r < rank:
+                mm.then_inc(sem["p%d" % r], 1)
+        for r in mine[:-1]:
+            finish(r)
+            te.wait_ge(sem["v%d" % r], 1)
+            te.matmul(acc(rank), weights[r], ycol(r), False, False)
+        te.wait_ge(sem.mg, 1)
+        wt("y3")
+        te.matmul(acc(rank), m3, ycol(3), False, True).then_inc(sem["p%d" % rank], 1)
+        finish(rank)
 
     if rank > 0:
         g.sync.wait_ge(sem["v%d" % rank], 1)
@@ -207,7 +290,7 @@ def rank_program(g, core, T, topo):
                 for it in _items(buf, lo, hi):
                     wg(it)
         transfers = []
-        for mask, lo, hi, ranks in _transfers(topo, cores, src, parts):
+        for mask, lo, hi, ranks in _transfers(topo, cores, src, parts, k in SPARE):
             ap = T[buf][:, lo:hi]
             ids = []
             for d in ranks:

@@ -2,31 +2,43 @@ from concourse.bass import DstId, RemoteDMATransfer
 from concourse.mybir import AluOpType
 
 N, W, TS = 8, 64, 128
+FO = W + 3 * TS
 
-SCRATCH = {"Y": ("sbuf", [128, N * W], "float32"), "acc0": ("psum", [128, 512], "float32")}
+SCRATCH = {"Y": ("sbuf", [128, N * W], "float32")}
 for _r in range(1, N):
     SCRATCH["R%d" % _r] = ("sbuf", [128, W + TS * _r], "float32")
     SCRATCH["acc%d" % _r] = ("psum", [128, 512], "float32")
 SCRATCH["ident"] = ("sbuf", [128, TS], "float32")
-SCRATCH["L5T"] = ("sbuf", [128, 3 * TS], "float32")
+SCRATCH["NAT"] = ("sbuf", [128, 2 * TS], "float32")
 SCRATCH["L6T"] = ("sbuf", [128, 3 * TS], "float32")
 SCRATCH["M7"] = ("sbuf", [128, 3 * TS], "float32")
 
 MSGS = [
-    (0, "Y", [(0, 64, [1, 2, 3, 7, 6])]),
-    (1, "R1", [(0, 192, [0, 2, 3])]),
-    (2, "R2", [(0, 320, [3, 1])]),
+    (0, "Y", [(0, 64, [1])], "spare"),
+    (0, "Y", [(0, 64, [2, 3, 7, 6])]),
+    (1, "R1", [(0, W, [0])], "spare"),
+    (1, "R1", [(0, 192, [2, 3])]),
+    (1, "R1", [(W, 192, [0])], "spare"),
+    (2, "R2", [(0, W, [3])], "spare"),
+    (2, "R2", [(0, 320, [1])]),
+    (2, "R2", [(W, 320, [3])], "spare"),
+    (3, "R3", [(0, W, [2])], "spare"),
     (3, "R3", [(0, 448, [1])]),
-    (3, "R3", [(0, 448, [2])]),
-    (4, "R4", [(0, 288, [7]), (288, 576, [6])]),
-    (4, "R4", [(0, 576, [5])]),
-    (5, "R5", [(0, 352, [7]), (352, 704, [6])]),
-    (6, "R6", [(0, 448, [7])]),
+    (3, "R3", [(W, 448, [2])], "spare"),
+    (4, "R4", [(0, W, [5])], "spare"),
+    (4, "R4", [(FO, FO + TS, [6, 7])]),
+    (4, "R4", [(0, FO, [6])]),
+    (4, "R4", [(W, FO + TS, [5])], "spare"),
+    (5, "R5", [(0, W, [7])]),
+    (5, "R5", [(FO, FO + 2 * TS, [6])]),
+    (5, "R5", [(W, FO, [7])]),
+    (6, "R6", [(0, W, [7])]),
     (6, "L6T", [(0, 384, [7])]),
-    (6, "R4", [(288, 576, [7])]),
-    (7, "R4", [(0, 288, [6])]),
-    (6, "R5", [(352, 704, [7])]),
-    (7, "R5", [(0, 352, [6])]),
+    (6, "R6", [(W, 448, [7])]),
+    (6, "R5", [(FO, FO + 2 * TS, [7])]),
+    (6, "R4", [(0, FO, [7])]),
+    (7, "R5", [(0, W, [6])]),
+    (7, "R5", [(W, FO, [6])]),
     (0, "Y", [(64, 128, [7, 6])]),
     (1, "Y", [(128, 192, [7])]),
     (7, "Y", [(128, 192, [6])]),
@@ -37,7 +49,6 @@ MSGS = [
     (2, "Y", [(192, 256, [5])]),
     (3, "Y", [(192, 256, [4])]),
 ]
-SPARE = (4,)
 
 ORDER = {
     0: [(1, 0)],
@@ -45,12 +56,12 @@ ORDER = {
     2: [(2, 0), (1, 0), (2, 1), (3, 0), (3, 1), (3, 2)],
     3: [(3, 0), (2, 0), (1, 0), (2, 1), (3, 1), (3, 2)],
     4: [(4, 0), (4, 1), (4, 2), (4, 3)],
-    5: [(4, 0), (5, 0), (4, 1), (4, 2), (5, 1), (5, 2), (4, 3), (5, 3), (5, 4)],
+    5: [],
     6: [],
     7: [],
 }
 
-SEMAPHORES = (["ld", "st", "sent", "id0", "id1", "tp", "tq", "tr", "lt", "lu", "lv", "pp", "qq", "qr", "hf", "mf", "mg"]
+SEMAPHORES = (["lb", "ld", "ln", "st", "sent", "id0", "id1", "tp", "lt", "pp", "qq", "qr", "hf", "mf", "mg"]
               + ["m%d" % k for k in range(len(MSGS))]
               + ["p%d" % r for r in range(1, N)] + ["v%d" % r for r in range(1, N)])
 
@@ -98,8 +109,12 @@ def rank_program(g, core, T, topo):
         return
     cores = T.cores
     sem = T.sem
+    te, ve, sub = g.tensor, g.vector, AluOpType.subtract
     have = {}
     piece = {}
+    owner = rank in (4, 5)
+    fold = rank >= 6
+    name = "R%d" % rank
 
     if rank == 0:
         g.sync.dma_start(T.Y[:, 0:W], T.b[:, :]).then_inc(sem.ld, 16)
@@ -107,16 +122,29 @@ def rank_program(g, core, T, topo):
         g.scalar.dma_start(T.y[:, :], T.b[:, :]).then_inc(sem.st, 16)
         g.scalar.wait_ge(sem.st, 16)
     else:
-        own = T["R%d" % rank]
-        g.sync.dma_start(own[:, 0:W], T.b[:, :]).then_inc(sem.ld, 16)
-        g.scalar.dma_start(own[:, W:W + TS * rank], T.l[:, 0:TS * rank]).then_inc(sem.ld, 16)
-        have["R%d" % rank] = [(sem.ld, 32)]
+        own = T[name]
+        last = 3 if owner else rank
+        g.sync.dma_start(own[:, 0:W], T.b[:, :]).then_inc(sem.lb, 16)
+        if owner:
+            g.scalar.dma_start(T.NAT[:, 0:TS * (rank - 3)], T.l[:, 3 * TS:rank * TS]).then_inc(sem.ln, 16)
+        g.scalar.dma_start(own[:, W:W + TS * last], T.l[:, 0:TS * last]).then_inc(sem.ld, 16)
+        have[name] = [(sem.lb, 16), (sem.ld, 16)]
 
-    for k, (src, buf, parts) in enumerate(MSGS):
-        for mask, lo, hi, ranks in _transfers(topo, cores, src, parts, k in SPARE):
+    def own_ready(lo, hi):
+        out = []
+        if lo < W:
+            out.append((sem.lb, 16))
+        if hi > W and lo < (FO if owner else W + TS * rank):
+            out.append((sem.ld, 16))
+        if owner and hi > FO:
+            out.append((sem.lt, 1))
+        return out
+
+    for k, msg in enumerate(MSGS):
+        for mask, lo, hi, ranks in _transfers(topo, cores, msg[0], msg[2], len(msg) > 3):
             if rank in ranks:
-                piece[(buf, lo, hi)] = (sem["m%d" % k], _ones(mask))
-                for it in _items(buf, lo, hi):
+                piece[(msg[1], lo, hi)] = (sem["m%d" % k], _ones(mask))
+                for it in _items(msg[1], lo, hi):
                     have.setdefault(it, []).append((sem["m%d" % k], _ones(mask)))
     order = ORDER[rank]
     size = {}
@@ -132,7 +160,6 @@ def rank_program(g, core, T, topo):
     have["ident"] = [(sem.id1, 1)]
     if rank == 6:
         have["L6T"] = [(sem.lt, 1)]
-    fold = rank >= 6
 
     def waiter(queue):
         seen = set()
@@ -144,7 +171,14 @@ def rank_program(g, core, T, topo):
                     queue.wait_ge(s, n)
         return wait
 
+    def landed(queue, buf, lo, hi):
+        for (b2, l2, h2), (s, n) in sorted(piece.items(), key=lambda kv: kv[0]):
+            if b2 == buf and l2 < hi and lo < h2:
+                queue.wait_ge(s, n)
+
     def tile(r, s):
+        if owner and r == rank and s >= 3:
+            return T.NAT[:, TS * (s - 3):TS * (s - 2)]
         return T["R%d" % r][:, W + TS * s:W + TS * (s + 1)]
 
     def ycol(s):
@@ -153,63 +187,75 @@ def rank_program(g, core, T, topo):
     def acc(r):
         return T["acc%d" % r][:, 0:W]
 
-    wt = waiter(g.tensor)
+    wt = waiter(te)
+    wv = waiter(ve)
+    eye = T.ident[:, :]
+    if owner or fold:
+        ve.memset(eye, 1.0).then_inc(sem.id0, 1)
+
+    if owner:
+        n_t = rank - 3
+        wt("ident")
+        te.wait_ge(sem.ln, 16)
+        for j in range(n_t):
+            blk = slice(TS * j, TS * (j + 1))
+            te.matmul(T.acc1[:, blk], T.NAT[:, blk], eye, True, True).then_inc(sem.tp, 1)
+        ve.wait_ge(sem.tp, n_t)
+        ve.tensor_copy(own[:, FO:FO + n_t * TS], T.acc1[:, 0:n_t * TS]).then_inc(sem.lt, 1)
+
     done = dict((r, 0) for r in rows)
     for r, s in order:
         wt("R%d" % r)
         wt("y%d" % s)
         done[r] += 1
-        mm = g.tensor.matmul(acc(r), tile(r, s), ycol(s), done[r] == 1, done[r] == size[r])
+        mm = te.matmul(acc(r), tile(r, s), ycol(s), done[r] == 1, done[r] == size[r])
         if done[r] == size[r]:
             mm.then_inc(sem["p%d" % r], 1)
 
-    wv = waiter(g.vector)
-
     def finish(r):
         wv("R%d" % r)
-        g.vector.wait_ge(sem["p%d" % r], 1)
-        g.vector.tensor_tensor(ycol(r), T["R%d" % r][:, 0:W], acc(r), AluOpType.subtract).then_inc(sem["v%d" % r], 1)
+        ve.wait_ge(sem["p%d" % r], 1)
+        ve.tensor_tensor(ycol(r), T["R%d" % r][:, 0:W], acc(r), sub).then_inc(sem["v%d" % r], 1)
 
     for r in rows:
         finish(r)
 
+    mine = list(range(4, rank + 1))
+    weights, m3 = {}, None
+
+    if rank == 5:
+        m3 = T.M7[:, 0:TS]
+        wt("R4")
+        te.matmul(T.acc2[:, 0:TS], T.R4[:, FO:FO + TS], tile(5, 4), True, True).then_inc(sem.qr, 1)
+        ve.wait_ge(sem.ln, 16)
+        ve.wait_ge(sem.qr, 1)
+        ve.tensor_tensor(m3, tile(5, 3), T.acc2[:, 0:TS], sub).then_inc(sem.mg, 1)
+        wt("R5")
+        wt("y0")
+        for r in mine:
+            te.matmul(acc(r), tile(r, 0), ycol(0), True, False)
+        wt("y1")
+        for r in mine:
+            te.matmul(acc(r), tile(r, 1), ycol(1), False, False)
+        weights = {4: tile(5, 4)}
+
     if fold:
-        te, ve, sub = g.tensor, g.vector, AluOpType.subtract
-        eye = T.ident[:, :]
-        t54T, t43T, t53T = T.L5T[:, 0:TS], T.L5T[:, TS:2 * TS], T.L5T[:, 2 * TS:3 * TS]
-        left4 = [key for key in piece if key[0] == "R4" and key[1] == 0][0]
-        left5 = [key for key in piece if key[0] == "R5" and key[1] == 0][0]
-        right4 = [key for key in piece if key[0] == "R4" and key[2] == W + 4 * TS][0]
-        right5 = [key for key in piece if key[0] == "R5" and key[2] == W + 5 * TS][0]
-        mine = list(range(4, rank + 1))
-        ve.memset(eye, 1.0).then_inc(sem.id0, 1)
+        t43T, t53T, t54T = tile(4, 3), tile(5, 3), tile(5, 4)
 
-        def transposes():
-            wt("ident")
-            te.wait_ge(*piece[right4])
-            te.matmul(T.acc3[:, 0:TS], tile(4, 3), eye, True, True).then_inc(sem.tq, 1)
-            te.wait_ge(*piece[right5])
-            te.matmul(T.acc0[:, 0:TS], tile(5, 4), eye, True, True).then_inc(sem.tr, 1)
-            te.matmul(T.acc3[:, TS:2 * TS], tile(5, 3), eye, True, True).then_inc(sem.tq, 1)
-            ve.wait_ge(sem.tr, 1)
-            ve.tensor_copy(t54T, T.acc0[:, 0:TS]).then_inc(sem.lu, 1)
-            ve.wait_ge(sem.tq, 2)
-            ve.tensor_copy(T.L5T[:, TS:3 * TS], T.acc3[:, 0:2 * TS]).then_inc(sem.lv, 1)
-
-        def fold_tiles(h5, h4, h4_in, m3, m3_in):
-            te.wait_ge(sem.lu, 1)
+        def fold_tiles(h5, h4, h4_in, m, m_in):
+            landed(te, "R5", FO, FO + 2 * TS)
             te.matmul(T.acc1[:, 0:TS], t54T, h5, True, True).then_inc(sem.qq, 1)
-            te.wait_ge(sem.lv, 1)
             te.matmul(T.acc2[:, 0:TS], t53T, h5, True, False)
+            landed(te, "R4", FO, FO + TS)
             te.wait_ge(sem.hf, 1)
             te.matmul(T.acc2[:, 0:TS], t43T, h4, False, True).then_inc(sem.qr, 1)
             ve.wait_ge(sem.qq, 1)
             ve.tensor_tensor(h4, h4_in, T.acc1[:, 0:TS], sub).then_inc(sem.hf, 1)
             ve.wait_ge(sem.qr, 1)
-            ve.tensor_tensor(m3, m3_in, T.acc2[:, 0:TS], sub).then_inc(sem.mg, 1)
+            ve.tensor_tensor(m, m_in, T.acc2[:, 0:TS], sub).then_inc(sem.mg, 1)
 
-        wt("R%d" % rank)
-        wv("R%d" % rank)
+        wt(name)
+        wv(name)
         if rank == 6:
             wt("ident")
             for s in (3, 4, 5):
@@ -219,15 +265,13 @@ def rank_program(g, core, T, topo):
             ve.tensor_copy(T.L6T[:, :], T.acc1[:, 0:3 * TS]).then_inc(sem.lt, 1)
             wt("y0")
             te.matmul(acc(6), tile(6, 0), ycol(0), True, False)
-            transposes()
             wt("L6T")
             h5, h4, m3 = tile(6, 5), T.M7[:, TS:2 * TS], T.M7[:, 0:TS]
             fold_tiles(h5, h4, tile(6, 4), m3, tile(6, 3))
             weights = {4: h4, 5: h5}
-            wt("R4")
-            te.matmul(acc(4), tile(4, 0), ycol(0), True, False)
-            wt("R5")
-            te.matmul(acc(5), tile(5, 0), ycol(0), True, False)
+            for r in (4, 5):
+                landed(te, "R%d" % r, 0, FO)
+                te.matmul(acc(r), tile(r, 0), ycol(0), True, False)
             wt("y1")
             for r in mine:
                 te.matmul(acc(r), tile(r, 1), ycol(1), False, False)
@@ -242,19 +286,19 @@ def rank_program(g, core, T, topo):
             te.matmul(acc(7), tile(7, 0), ycol(0), True, False)
             wt("R6")
             te.matmul(acc(6), tile(6, 0), ycol(0), True, False)
-            te.wait_ge(*piece[left4])
-            te.matmul(acc(4), tile(4, 0), ycol(0), True, False)
-            te.wait_ge(*piece[left5])
-            te.matmul(acc(5), tile(5, 0), ycol(0), True, False)
             wt("y1")
-            for r in (5, 6, 7):
+            for r in (6, 7):
                 te.matmul(acc(r), tile(r, 1), ycol(1), False, False)
-            transposes()
-            te.matmul(acc(4), tile(4, 1), ycol(1), False, False)
             te.wait_ge(sem.mf, 1)
             m3, h4, h5 = T.M7[:, 0:TS], T.M7[:, TS:2 * TS], T.M7[:, 2 * TS:3 * TS]
             fold_tiles(h5, h4, h4, m3, m3)
             weights = {4: h4, 5: h5, 6: tile(7, 6)}
+            for r in (5, 4):
+                landed(te, "R%d" % r, 0, FO)
+                te.matmul(acc(r), tile(r, 0), ycol(0), True, False)
+                te.matmul(acc(r), tile(r, 1), ycol(1), False, False)
+
+    if rank >= 5:
         wt("y2")
         for r in mine:
             mm = te.matmul(acc(r), tile(r, 2), ycol(2), False, r < rank)
@@ -274,23 +318,26 @@ def rank_program(g, core, T, topo):
         g.sync.dma_start(T.y[:, :], T.Y[:, W * rank:W * (rank + 1)]).then_inc(sem.st, 16)
         g.sync.wait_ge(sem.st, 16)
 
-    if fold:
+    if owner or fold:
         g.wait_ge(sem.id0, 1)
         g.affine_select(T.ident[:, :], T.ident[:, :], [[-1, TS]], AluOpType.is_equal, 0.0, 0, 1).then_inc(sem.id1, 1)
     wg = waiter(g)
     sent = 0
-    for k, (src, buf, parts) in enumerate(MSGS):
+    for k, msg in enumerate(MSGS):
+        src, buf, parts = msg[0], msg[1], msg[2]
         if src != rank:
             continue
         for lo, hi, _ in parts:
-            if (buf, lo, hi) in piece:
-                s, n = piece[(buf, lo, hi)]
-                g.wait_ge(s, n)
+            if buf == name:
+                for s, n in own_ready(lo, hi):
+                    g.wait_ge(s, n)
+            elif buf.startswith("R") or (buf, lo, hi) in piece:
+                landed(g, buf, lo, hi)
             else:
                 for it in _items(buf, lo, hi):
                     wg(it)
         transfers = []
-        for mask, lo, hi, ranks in _transfers(topo, cores, src, parts, k in SPARE):
+        for mask, lo, hi, ranks in _transfers(topo, cores, src, parts, len(msg) > 3):
             ap = T[buf][:, lo:hi]
             ids = []
             for d in ranks:

from concourse.bass import DstId, RemoteDMATransfer
from concourse.mybir import AluOpType

N, W, TS = 8, 64, 128
FO = W + 3 * TS

SCRATCH = {"Y": ("sbuf", [128, N * W], "float32")}
for _r in range(1, N):
    SCRATCH["R%d" % _r] = ("sbuf", [128, W + TS * _r], "float32")
    SCRATCH["acc%d" % _r] = ("psum", [128, 512], "float32")
SCRATCH["ident"] = ("sbuf", [128, TS], "float32")
SCRATCH["NAT"] = ("sbuf", [128, 2 * TS], "float32")
SCRATCH["L6T"] = ("sbuf", [128, 3 * TS], "float32")
SCRATCH["M7"] = ("sbuf", [128, 3 * TS], "float32")

MSGS = [
    (0, "Y", [(0, 64, [1])], "spare"),
    (0, "Y", [(0, 64, [2, 3, 7, 6])]),
    (1, "R1", [(0, W, [0])], "spare"),
    (1, "R1", [(0, 192, [2, 3])]),
    (1, "R1", [(W, 192, [0])], "spare"),
    (2, "R2", [(0, W, [3])], "spare"),
    (2, "R2", [(0, 320, [1])]),
    (2, "R2", [(W, 320, [3])], "spare"),
    (3, "R3", [(0, W, [2])], "spare"),
    (3, "R3", [(0, 448, [1])]),
    (3, "R3", [(W, 448, [2])], "spare"),
    (4, "R4", [(0, W, [5])], "spare"),
    (4, "R4", [(FO, FO + TS, [6, 7])]),
    (4, "R4", [(0, FO, [6])]),
    (4, "R4", [(W, FO + TS, [5])], "spare"),
    (5, "R5", [(0, W, [7])]),
    (5, "R5", [(FO, FO + 2 * TS, [6])]),
    (5, "R5", [(W, FO, [7])]),
    (6, "R6", [(0, W, [7])]),
    (6, "L6T", [(0, 384, [7])]),
    (6, "R6", [(W, 448, [7])]),
    (6, "R5", [(FO, FO + 2 * TS, [7])]),
    (6, "R4", [(0, FO, [7])]),
    (7, "R5", [(0, W, [6])]),
    (7, "R5", [(W, FO, [6])]),
    (0, "Y", [(64, 128, [7, 6])]),
    (1, "Y", [(128, 192, [7])]),
    (7, "Y", [(128, 192, [6])]),
    (1, "Y", [(192, 256, [7, 6])]),
    (3, "Y", [(0, 64, [5, 4])]),
    (2, "Y", [(64, 192, [5])]),
    (5, "Y", [(64, 192, [4])]),
    (2, "Y", [(192, 256, [5])]),
    (3, "Y", [(192, 256, [4])]),
]

ORDER = {
    0: [(1, 0)],
    1: [(1, 0), (2, 0), (2, 1), (3, 0), (3, 1), (3, 2)],
    2: [(2, 0), (1, 0), (2, 1), (3, 0), (3, 1), (3, 2)],
    3: [(3, 0), (2, 0), (1, 0), (2, 1), (3, 1), (3, 2)],
    4: [(4, 0), (4, 1), (4, 2), (4, 3)],
    5: [],
    6: [],
    7: [],
}

SEMAPHORES = (["lb", "ld", "ln", "st", "sent", "id0", "id1", "tp", "lt", "pp", "qq", "qr", "hf", "mf", "mg"]
              + ["m%d" % k for k in range(len(MSGS))]
              + ["p%d" % r for r in range(1, N)] + ["v%d" % r for r in range(1, N)])


def _items(buf, lo, hi):
    if buf == "Y":
        return ["y%d" % s for s in range(lo // W, hi // W)]
    return [buf]


def _ones(mask):
    return bin(mask).count("1")


def _transfers(topo, cores, src, parts, spare):
    c = cores[src]

    def near(d):
        return (topo.host(cores[d]), topo.chip(cores[d])) == (topo.host(c), topo.chip(c))

    m_off = 0
    far = [d for _, _, dests in parts for d in dests if not near(d)]
    if spare:
        far = [d for d in range(len(cores)) if not near(d) and topo.may_write(c, cores[d])]
    if far:
        m_off = topo.mask(c, cores[far[0]])
        for d in far:
            m_off &= topo.mask(c, cores[d])
    bits = [1 << i for i in range(m_off.bit_length()) if (m_off >> i) & 1]
    share = len(bits) // len(parts)
    out = []
    for j, (lo, hi, dests) in enumerate(parts):
        on = [d for d in dests if near(d)]
        off = [d for d in dests if not near(d)]
        if on:
            out.append((topo.mask(c, cores[on[0]]) & ~m_off, lo, hi, on))
        if off:
            out.append((sum(bits[j * share:(j + 1) * share]), lo, hi, off))
    return out


def rank_program(g, core, T, topo):
    rank = T.rank_of(core)
    if rank is None:
        return
    cores = T.cores
    sem = T.sem
    te, ve, sub = g.tensor, g.vector, AluOpType.subtract
    have = {}
    piece = {}
    owner = rank in (4, 5)
    fold = rank >= 6
    name = "R%d" % rank

    if rank == 0:
        g.sync.dma_start(T.Y[:, 0:W], T.b[:, :]).then_inc(sem.ld, 16)
        have["y0"] = [(sem.ld, 16)]
        g.scalar.dma_start(T.y[:, :], T.b[:, :]).then_inc(sem.st, 16)
        g.scalar.wait_ge(sem.st, 16)
    else:
        own = T[name]
        last = 3 if owner else rank
        g.sync.dma_start(own[:, 0:W], T.b[:, :]).then_inc(sem.lb, 16)
        if owner:
            g.scalar.dma_start(T.NAT[:, 0:TS * (rank - 3)], T.l[:, 3 * TS:rank * TS]).then_inc(sem.ln, 16)
        g.scalar.dma_start(own[:, W:W + TS * last], T.l[:, 0:TS * last]).then_inc(sem.ld, 16)
        have[name] = [(sem.lb, 16), (sem.ld, 16)]

    def own_ready(lo, hi):
        out = []
        if lo < W:
            out.append((sem.lb, 16))
        if hi > W and lo < (FO if owner else W + TS * rank):
            out.append((sem.ld, 16))
        if owner and hi > FO:
            out.append((sem.lt, 1))
        return out

    for k, msg in enumerate(MSGS):
        for mask, lo, hi, ranks in _transfers(topo, cores, msg[0], msg[2], len(msg) > 3):
            if rank in ranks:
                piece[(msg[1], lo, hi)] = (sem["m%d" % k], _ones(mask))
                for it in _items(msg[1], lo, hi):
                    have.setdefault(it, []).append((sem["m%d" % k], _ones(mask)))
    order = ORDER[rank]
    size = {}
    for r, _ in order:
        size[r] = size.get(r, 0) + 1
    rows, cnt = [], {}
    for r, _ in order:
        cnt[r] = cnt.get(r, 0) + 1
        if cnt[r] == size[r]:
            rows.append(r)
    for r in rows:
        have["y%d" % r] = [(sem["v%d" % r], 1)]
    have["ident"] = [(sem.id1, 1)]
    if rank == 6:
        have["L6T"] = [(sem.lt, 1)]

    def waiter(queue):
        seen = set()

        def wait(item):
            if item not in seen:
                seen.add(item)
                for s, n in have[item]:
                    queue.wait_ge(s, n)
        return wait

    def landed(queue, buf, lo, hi):
        for (b2, l2, h2), (s, n) in sorted(piece.items(), key=lambda kv: kv[0]):
            if b2 == buf and l2 < hi and lo < h2:
                queue.wait_ge(s, n)

    def tile(r, s):
        if owner and r == rank and s >= 3:
            return T.NAT[:, TS * (s - 3):TS * (s - 2)]
        return T["R%d" % r][:, W + TS * s:W + TS * (s + 1)]

    def ycol(s):
        return T.Y[:, W * s:W * (s + 1)]

    def acc(r):
        return T["acc%d" % r][:, 0:W]

    wt = waiter(te)
    wv = waiter(ve)
    eye = T.ident[:, :]
    if owner or fold:
        ve.memset(eye, 1.0).then_inc(sem.id0, 1)

    if owner:
        n_t = rank - 3
        wt("ident")
        te.wait_ge(sem.ln, 16)
        for j in range(n_t):
            blk = slice(TS * j, TS * (j + 1))
            te.matmul(T.acc1[:, blk], T.NAT[:, blk], eye, True, True).then_inc(sem.tp, 1)
        ve.wait_ge(sem.tp, n_t)
        ve.tensor_copy(own[:, FO:FO + n_t * TS], T.acc1[:, 0:n_t * TS]).then_inc(sem.lt, 1)

    done = dict((r, 0) for r in rows)
    for r, s in order:
        wt("R%d" % r)
        wt("y%d" % s)
        done[r] += 1
        mm = te.matmul(acc(r), tile(r, s), ycol(s), done[r] == 1, done[r] == size[r])
        if done[r] == size[r]:
            mm.then_inc(sem["p%d" % r], 1)

    def finish(r):
        wv("R%d" % r)
        ve.wait_ge(sem["p%d" % r], 1)
        ve.tensor_tensor(ycol(r), T["R%d" % r][:, 0:W], acc(r), sub).then_inc(sem["v%d" % r], 1)

    for r in rows:
        finish(r)

    mine = list(range(4, rank + 1))
    weights, m3 = {}, None

    if rank == 5:
        m3 = T.M7[:, 0:TS]
        wt("R4")
        te.matmul(T.acc2[:, 0:TS], T.R4[:, FO:FO + TS], tile(5, 4), True, True).then_inc(sem.qr, 1)
        ve.wait_ge(sem.ln, 16)
        ve.wait_ge(sem.qr, 1)
        ve.tensor_tensor(m3, tile(5, 3), T.acc2[:, 0:TS], sub).then_inc(sem.mg, 1)
        wt("R5")
        wt("y0")
        for r in mine:
            te.matmul(acc(r), tile(r, 0), ycol(0), True, False)
        wt("y1")
        for r in mine:
            te.matmul(acc(r), tile(r, 1), ycol(1), False, False)
        weights = {4: tile(5, 4)}

    if fold:
        t43T, t53T, t54T = tile(4, 3), tile(5, 3), tile(5, 4)

        def fold_tiles(h5, h4, h4_in, m, m_in):
            landed(te, "R5", FO, FO + 2 * TS)
            te.matmul(T.acc1[:, 0:TS], t54T, h5, True, True).then_inc(sem.qq, 1)
            te.matmul(T.acc2[:, 0:TS], t53T, h5, True, False)
            landed(te, "R4", FO, FO + TS)
            te.wait_ge(sem.hf, 1)
            te.matmul(T.acc2[:, 0:TS], t43T, h4, False, True).then_inc(sem.qr, 1)
            ve.wait_ge(sem.qq, 1)
            ve.tensor_tensor(h4, h4_in, T.acc1[:, 0:TS], sub).then_inc(sem.hf, 1)
            ve.wait_ge(sem.qr, 1)
            ve.tensor_tensor(m, m_in, T.acc2[:, 0:TS], sub).then_inc(sem.mg, 1)

        wt(name)
        wv(name)
        if rank == 6:
            wt("ident")
            for s in (3, 4, 5):
                blk = slice(TS * (s - 3), TS * (s - 2))
                te.matmul(T.acc1[:, blk], tile(6, s), eye, True, True).then_inc(sem.tp, 1)
            ve.wait_ge(sem.tp, 3)
            ve.tensor_copy(T.L6T[:, :], T.acc1[:, 0:3 * TS]).then_inc(sem.lt, 1)
            wt("y0")
            te.matmul(acc(6), tile(6, 0), ycol(0), True, False)
            wt("L6T")
            h5, h4, m3 = tile(6, 5), T.M7[:, TS:2 * TS], T.M7[:, 0:TS]
            fold_tiles(h5, h4, tile(6, 4), m3, tile(6, 3))
            weights = {4: h4, 5: h5}
            for r in (4, 5):
                landed(te, "R%d" % r, 0, FO)
                te.matmul(acc(r), tile(r, 0), ycol(0), True, False)
            wt("y1")
            for r in mine:
                te.matmul(acc(r), tile(r, 1), ycol(1), False, False)
        else:
            wt("L6T")
            for s in (3, 4, 5):
                blk = slice(TS * (s - 3), TS * (s - 2))
                te.matmul(T.acc2[:, blk], T.L6T[:, blk], tile(7, 6), True, True).then_inc(sem.pp, 1)
            ve.wait_ge(sem.pp, 3)
            ve.tensor_tensor(T.M7[:, :], T.R7[:, W + 3 * TS:W + 6 * TS], T.acc2[:, 0:3 * TS], sub).then_inc(sem.mf, 1)
            wt("y0")
            te.matmul(acc(7), tile(7, 0), ycol(0), True, False)
            wt("R6")
            te.matmul(acc(6), tile(6, 0), ycol(0), True, False)
            wt("y1")
            for r in (6, 7):
                te.matmul(acc(r), tile(r, 1), ycol(1), False, False)
            te.wait_ge(sem.mf, 1)
            m3, h4, h5 = T.M7[:, 0:TS], T.M7[:, TS:2 * TS], T.M7[:, 2 * TS:3 * TS]
            fold_tiles(h5, h4, h4, m3, m3)
            weights = {4: h4, 5: h5, 6: tile(7, 6)}
            for r in (5, 4):
                landed(te, "R%d" % r, 0, FO)
                te.matmul(acc(r), tile(r, 0), ycol(0), True, False)
                te.matmul(acc(r), tile(r, 1), ycol(1), False, False)

    if rank >= 5:
        wt("y2")
        for r in mine:
            mm = te.matmul(acc(r), tile(r, 2), ycol(2), False, r < rank)
            if r < rank:
                mm.then_inc(sem["p%d" % r], 1)
        for r in mine[:-1]:
            finish(r)
            te.wait_ge(sem["v%d" % r], 1)
            te.matmul(acc(rank), weights[r], ycol(r), False, False)
        te.wait_ge(sem.mg, 1)
        wt("y3")
        te.matmul(acc(rank), m3, ycol(3), False, True).then_inc(sem["p%d" % rank], 1)
        finish(rank)

    if rank > 0:
        g.sync.wait_ge(sem["v%d" % rank], 1)
        g.sync.dma_start(T.y[:, :], T.Y[:, W * rank:W * (rank + 1)]).then_inc(sem.st, 16)
        g.sync.wait_ge(sem.st, 16)

    if owner or fold:
        g.wait_ge(sem.id0, 1)
        g.affine_select(T.ident[:, :], T.ident[:, :], [[-1, TS]], AluOpType.is_equal, 0.0, 0, 1).then_inc(sem.id1, 1)
    wg = waiter(g)
    sent = 0
    for k, msg in enumerate(MSGS):
        src, buf, parts = msg[0], msg[1], msg[2]
        if src != rank:
            continue
        for lo, hi, _ in parts:
            if buf == name:
                for s, n in own_ready(lo, hi):
                    g.wait_ge(s, n)
            elif buf.startswith("R") or (buf, lo, hi) in piece:
                landed(g, buf, lo, hi)
            else:
                for it in _items(buf, lo, hi):
                    wg(it)
        transfers = []
        for mask, lo, hi, ranks in _transfers(topo, cores, src, parts, len(msg) > 3):
            ap = T[buf][:, lo:hi]
            ids = []
            for d in ranks:
                rid, pid = topo.addr(cores[d], core)
                ids.append(DstId(rid=rid, pnc=pid))
            transfers.append(RemoteDMATransfer(dst_ids=ids, dma_engine_mask=mask, remote_sem=sem["m%d" % k],
                                               srcs=[ap], dsts=[ap for _ in ranks], alu_op=0))
            sent += _ones(mask)
        g.remote_dma_fused(transfers, local_sem=sem.sent)
    if sent:
        g.wait_ge(sem.sent, sent)
